import numpy as np
import ml_dtypes

BF16 = ml_dtypes.bfloat16


def bf(x):
    return np.asarray(x, np.float32).astype(BF16)


def f32(x):
    return np.asarray(x, np.float32)


def f64(x):
    return np.asarray(x).astype(np.float64)


def striped(idx):
    return np.concatenate([l.reshape(-1, 16).T for l in idx])


def rows(idx, k):
    return np.tile(np.repeat(idx, 16, axis=0), (k // (16 * 8), 1))


def look(tab, idx):
    return np.take_along_axis(f64(tab), rows(idx, len(tab)), axis=1)


K, S, V, N, M = 128, 2048, 1024, 1024, 128


def setup_inputs():
    return {"tab": f32(np.random.standard_normal((2, K, S))), "y": f32(np.random.standard_normal((K, V))), "w": bf(np.random.standard_normal((K, M)) / np.sqrt(K)), "b": f32(0.5 * np.random.standard_normal((M, 1))), "offs": striped(np.stack([np.random.permutation(S)[:N] for _ in range(8)]))}


def reference(tab, y, w, b, offs):
    idx = np.stack([g.T.reshape(-1) for g in np.split(offs, 8)])
    x = (look(tab[0], idx) - f64(y)) * (np.maximum(look(tab[1], idx), 0.0))
    return np.maximum(f64(w).T @ x + f64(b), 0.0)

@@ -1,0 +1,48 @@
+import concourse.mybir as mybir
+
+F32, BF16, U16 = mybir.dt.float32, mybir.dt.bfloat16, mybir.dt.uint16
+SUB, MULT = mybir.AluOpType.subtract, mybir.AluOpType.mult
+RELU = mybir.ActivationFunctionType.Relu
+
+ROWS, PLACES, N, M = 128, 2048, 1024, 128
+PIECE = 512
+GROUP = 16
+
+FLOPS = 2 * ROWS * M * N
+
+
+def tile_lookup_vg_subrelu_relu_kernel(tc, tab, y, w, b, offs, out):
+    nc = tc.nc
+    with (
+        tc.tile_pool(name="held", bufs=1) as held,
+        tc.tile_pool(name="work", bufs=N // PIECE) as work,
+        tc.psum_pool(name="psum", bufs=N // PIECE) as psum,
+    ):
+        offsets = held.tile([ROWS, N // GROUP], U16)
+        values = held.tile([ROWS, PLACES], F32)
+        gates = held.tile([ROWS, PLACES], F32)
+        stream = [held.tile([ROWS, PIECE], F32, name=f"stream{p}") for p in range(N // PIECE)]
+        weights = held.tile([ROWS, M], BF16)
+        bias = held.tile([M, 1], F32)
+
+        nc.sync.dma_start(offsets[:], offs)
+        nc.sync.dma_start(values[:], tab[0])
+        nc.sync.dma_start(stream[0][:], y[:, :PIECE])
+        nc.sync.dma_start(gates[:], tab[1])
+        nc.sync.dma_start(stream[1][:], y[:, PIECE:])
+        nc.scalar.dma_start(weights[:], w)
+        nc.scalar.dma_start(bias[:], b)
+
+        for p in range(N // PIECE):
+            entries = offsets[:, p * PIECE // GROUP : (p + 1) * PIECE // GROUP]
+            diff = work.tile([ROWS, PIECE], F32)
+            gate = work.tile([ROWS, PIECE], F32)
+            x = work.tile([ROWS, PIECE], BF16)
+            acc = psum.tile([M, PIECE], F32)
+            res = work.tile([M, PIECE], F32)
+            nc.vector.tensor_tensor(diff[:], values[:].indirect(entries), stream[p][:], SUB)
+            nc.scalar.activation(gate[:], gates[:].indirect(entries), RELU)
+            nc.vector.tensor_tensor(x[:], diff[:], gate[:], MULT)
+            nc.tensor.matmul(acc[:], weights[:], x[:], start=True, stop=True)
+            nc.scalar.activation(res[:], acc[:], RELU, bias=bias[:])
+            nc.sync.dma_start(out[:, p * PIECE : (p + 1) * PIECE], res[:])

@@ -1,12 +1,14 @@
 import concourse.mybir as mybir
 
 F32, BF16, U16 = mybir.dt.float32, mybir.dt.bfloat16, mybir.dt.uint16
-SUB, MULT = mybir.AluOpType.subtract, mybir.AluOpType.mult
+ADD, SUB, MULT, MAX = mybir.AluOpType.add, mybir.AluOpType.subtract, mybir.AluOpType.mult, mybir.AluOpType.max
 RELU = mybir.ActivationFunctionType.Relu
 
 ROWS, PLACES, N, M = 128, 2048, 1024, 128
-PIECE = 512
 GROUP = 16
+PIECE = 512
+CHUNK = 256
+PIECES, CHUNKS = N // PIECE, N // CHUNK
 
 FLOPS = 2 * ROWS * M * N
 
@@ -15,13 +17,15 @@ def tile_lookup_vg_subrelu_relu_kernel(tc, tab, y, w, b, offs, out):
     nc = tc.nc
     with (
         tc.tile_pool(name="held", bufs=1) as held,
-        tc.tile_pool(name="work", bufs=N // PIECE) as work,
-        tc.psum_pool(name="psum", bufs=N // PIECE) as psum,
+        tc.tile_pool(name="work", bufs=CHUNKS) as work,
+        tc.psum_pool(name="psum", bufs=CHUNKS) as psum,
     ):
         offsets = held.tile([ROWS, N // GROUP], U16)
         values = held.tile([ROWS, PLACES], F32)
         gates = held.tile([ROWS, PLACES], F32)
-        stream = [held.tile([ROWS, PIECE], F32, name=f"stream{p}") for p in range(N // PIECE)]
+        stream = [held.tile([ROWS, PIECE], F32, name=f"stream{p}") for p in range(PIECES)]
+        diff = [held.tile([ROWS, PIECE], F32, name=f"diff{p}") for p in range(PIECES)]
+        gate = [held.tile([ROWS, PIECE], F32, name=f"gate{p}") for p in range(PIECES)]
         weights = held.tile([ROWS, M], BF16)
         bias = held.tile([M, 1], F32)
 
@@ -33,16 +37,24 @@ def tile_lookup_vg_subrelu_relu_kernel(tc, tab, y, w, b, offs, out):
         nc.scalar.dma_start(weights[:], w)
         nc.scalar.dma_start(bias[:], b)
 
-        for p in range(N // PIECE):
+        warm = held.tile([ROWS, 1], F32)
+        nc.vector.memset(warm[:], 0.0)
+        nc.scalar.activation(warm[:], warm[:], RELU)
+
+        for p in range(PIECES):
             entries = offsets[:, p * PIECE // GROUP : (p + 1) * PIECE // GROUP]
-            diff = work.tile([ROWS, PIECE], F32)
-            gate = work.tile([ROWS, PIECE], F32)
-            x = work.tile([ROWS, PIECE], BF16)
-            acc = psum.tile([M, PIECE], F32)
-            res = work.tile([M, PIECE], F32)
-            nc.vector.tensor_tensor(diff[:], values[:].indirect(entries), stream[p][:], SUB)
-            nc.scalar.activation(gate[:], gates[:].indirect(entries), RELU)
-            nc.vector.tensor_tensor(x[:], diff[:], gate[:], MULT)
+            nc.vector.tensor_tensor(diff[p][:], values[:].indirect(entries), stream[p][:], SUB)
+            nc.scalar.activation(gate[p][:], gates[:].indirect(entries), RELU)
+
+        for c in range(CHUNKS):
+            p, start = divmod(c * CHUNK, PIECE)
+            x = work.tile([ROWS, CHUNK], BF16)
+            acc = psum.tile([M, CHUNK], F32)
+            res = work.tile([M, CHUNK], F32)
+            nc.vector.tensor_tensor(x[:], diff[p][:, start : start + CHUNK], gate[p][:, start : start + CHUNK], MULT)
             nc.tensor.matmul(acc[:], weights[:], x[:], start=True, stop=True)
-            nc.scalar.activation(res[:], acc[:], RELU, bias=bias[:])
-            nc.sync.dma_start(out[:, p * PIECE : (p + 1) * PIECE], res[:])
+            if c < CHUNKS - 1:
+                nc.scalar.activation(res[:], acc[:], RELU, bias=bias[:])
+            else:
+                nc.vector.tensor_scalar(res[:], acc[:], bias[:], 0.0, ADD, MAX)
+            nc.sync.dma_start(out[:, c * CHUNK : (c + 1) * CHUNK], res[:])

@@ -7,7 +7,7 @@ RELU = mybir.ActivationFunctionType.Relu
 ROWS, PLACES, N, M = 128, 2048, 1024, 128
 GROUP = 16
 PIECE = 512
-CHUNK = 256
+CHUNK = 128
 PIECES, CHUNKS = N // PIECE, N // CHUNK
 
 FLOPS = 2 * ROWS * M * N
@@ -29,13 +29,13 @@ def tile_lookup_vg_subrelu_relu_kernel(tc, tab, y, w, b, offs, out):
         weights = held.tile([ROWS, M], BF16)
         bias = held.tile([M, 1], F32)
 
-        nc.sync.dma_start(offsets[:], offs)
         nc.sync.dma_start(values[:], tab[0])
+        nc.sync.dma_start(offsets[:], offs)
         nc.sync.dma_start(stream[0][:], y[:, :PIECE])
         nc.sync.dma_start(gates[:], tab[1])
         nc.sync.dma_start(stream[1][:], y[:, PIECE:])
-        nc.scalar.dma_start(weights[:], w)
-        nc.scalar.dma_start(bias[:], b)
+        nc.sync.dma_start(weights[:], w)
+        nc.sync.dma_start(bias[:], b)
 
         warm = held.tile([ROWS, 1], F32)
         nc.vector.memset(warm[:], 0.0)
@@ -53,7 +53,7 @@ def tile_lookup_vg_subrelu_relu_kernel(tc, tab, y, w, b, offs, out):
             res = work.tile([M, CHUNK], F32)
             nc.vector.tensor_tensor(x[:], diff[p][:, start : start + CHUNK], gate[p][:, start : start + CHUNK], MULT)
             nc.tensor.matmul(acc[:], weights[:], x[:], start=True, stop=True)
-            if c < CHUNKS - 1:
+            if c < CHUNKS - 2:
                 nc.scalar.activation(res[:], acc[:], RELU, bias=bias[:])
             else:
                 nc.vector.tensor_scalar(res[:], acc[:], bias[:], 0.0, ADD, MAX)

import concourse.mybir as mybir

F32, BF16, U16 = mybir.dt.float32, mybir.dt.bfloat16, mybir.dt.uint16
ADD, SUB, MULT, MAX = mybir.AluOpType.add, mybir.AluOpType.subtract, mybir.AluOpType.mult, mybir.AluOpType.max
RELU = mybir.ActivationFunctionType.Relu

ROWS, PLACES, N, M = 128, 2048, 1024, 128
GROUP = 16
PIECE = 512
CHUNK = 128
PIECES, CHUNKS = N // PIECE, N // CHUNK

FLOPS = 2 * ROWS * M * N


def tile_lookup_vg_subrelu_relu_kernel(tc, tab, y, w, b, offs, out):
    nc = tc.nc
    with (
        tc.tile_pool(name="held", bufs=1) as held,
        tc.tile_pool(name="work", bufs=CHUNKS) as work,
        tc.psum_pool(name="psum", bufs=CHUNKS) as psum,
    ):
        offsets = held.tile([ROWS, N // GROUP], U16)
        values = held.tile([ROWS, PLACES], F32)
        gates = held.tile([ROWS, PLACES], F32)
        stream = [held.tile([ROWS, PIECE], F32, name=f"stream{p}") for p in range(PIECES)]
        diff = [held.tile([ROWS, PIECE], F32, name=f"diff{p}") for p in range(PIECES)]
        gate = [held.tile([ROWS, PIECE], F32, name=f"gate{p}") for p in range(PIECES)]
        weights = held.tile([ROWS, M], BF16)
        bias = held.tile([M, 1], F32)

        nc.sync.dma_start(values[:], tab[0])
        nc.sync.dma_start(offsets[:], offs)
        nc.sync.dma_start(stream[0][:], y[:, :PIECE])
        nc.sync.dma_start(gates[:], tab[1])
        nc.sync.dma_start(stream[1][:], y[:, PIECE:])
        nc.sync.dma_start(weights[:], w)
        nc.sync.dma_start(bias[:], b)

        warm = held.tile([ROWS, 1], F32)
        nc.vector.memset(warm[:], 0.0)
        nc.scalar.activation(warm[:], warm[:], RELU)

        for p in range(PIECES):
            entries = offsets[:, p * PIECE // GROUP : (p + 1) * PIECE // GROUP]
            nc.vector.tensor_tensor(diff[p][:], values[:].indirect(entries), stream[p][:], SUB)
            nc.scalar.activation(gate[p][:], gates[:].indirect(entries), RELU)

        for c in range(CHUNKS):
            p, start = divmod(c * CHUNK, PIECE)
            x = work.tile([ROWS, CHUNK], BF16)
            acc = psum.tile([M, CHUNK], F32)
            res = work.tile([M, CHUNK], F32)
            nc.vector.tensor_tensor(x[:], diff[p][:, start : start + CHUNK], gate[p][:, start : start + CHUNK], MULT)
            nc.tensor.matmul(acc[:], weights[:], x[:], start=True, stop=True)
            if c < CHUNKS - 2:
                nc.scalar.activation(res[:], acc[:], RELU, bias=bias[:])
            else:
                nc.vector.tensor_scalar(res[:], acc[:], bias[:], 0.0, ADD, MAX)
            nc.sync.dma_start(out[:, c * CHUNK : (c + 1) * CHUNK], res[:])
